import numpy as np
import ml_dtypes


def mxq(x, axis, fmt="e4m3"):
    dtype, down = {"e4m3": (ml_dtypes.float8_e4m3fn, 7), "e5m2": (ml_dtypes.float8_e5m2, 14)}[fmt]
    v = np.moveaxis(np.asarray(x, np.float32).astype(ml_dtypes.bfloat16).astype(np.float64), axis, -1)
    blocks = v.reshape(v.shape[:-1] + (-1, 32))
    amax = np.abs(blocks).max(-1, keepdims=True)
    byte = np.maximum(np.where(amax > 0, np.frexp(amax)[1] - 1 + 127, 0) - down, 1)
    scale = np.exp2(byte - 127.0)
    codes = (blocks / scale).astype(np.float32).astype(dtype).astype(np.float64)
    return np.moveaxis((codes * scale).reshape(v.shape), -1, axis)


WIDE = False


def mx_kscale(k):
    if not WIDE:
        return np.ones(k)
    levels = np.array([10, -10, 5, -5, 0])
    if k % 512:
        return np.exp2(np.random.permutation(np.resize(levels, k // 32))).repeat(32)
    a = np.empty((k // 512, 16))
    for p in range(k // 512):
        a[p, :8] = np.random.permutation(np.resize(levels, 8))
        for g in range(8):
            far = levels[np.abs(levels - a[p, g]) >= 10]
            a[p, g + 8] = far[np.random.randint(len(far))]
    return np.exp2(a.ravel()).repeat(32)


def f64(x):
    return np.asarray(x).astype(np.float64)


def striped8(idx):
    return np.asarray(idx).reshape(8, -1, 16).transpose(0, 2, 1).reshape(128, -1).astype(np.uint16)


def unstriped8(offs):
    return offs.reshape(8, 16, -1).transpose(0, 2, 1).reshape(8, -1).astype(np.int64)


def pick8(x, idx, run):
    r = np.arange(len(x))
    return x[r[:, None], idx[r % (8 * run) // run]]


E2M1 = np.array([0.0, 0.5, 1.0, 1.5, 2.0, 3.0, 4.0, 6.0, -0.0, -0.5, -1.0, -1.5, -2.0, -3.0, -4.0, -6.0])


def pack_weight(w, fmt):
    k, n = w.shape
    w = f64(np.asarray(w, np.float32).astype(ml_dtypes.bfloat16)).reshape(k // 32, 32, n)
    amax = np.abs(w).max(1)
    if fmt == "e4m3":
        byte = np.frexp(amax)[1] - 1 + 127 - 7
    else:
        mant, ex = np.frexp(amax / 6.0)
        byte = np.where(mant > 0.5, ex, ex - 1) + 127
    byte = np.clip(np.where(amax > 0, byte, 1), 1, 254)
    scaled = (w * np.exp2(127.0 - byte)[:, None, :]).reshape(k, n).astype(np.float32)
    by_word = np.ascontiguousarray(scaled.reshape(k // 512, 128, 4, n).transpose(0, 1, 3, 2))
    if fmt == "e4m3":
        words = by_word.astype(ml_dtypes.float8_e4m3fn).view(np.uint8)
    else:
        c = by_word.astype(ml_dtypes.float4_e2m1fn).view(np.uint8) & 0xF
        words = (c[..., 0::2] | (c[..., 1::2] << 4)).reshape(k // 512, 128, 2 * n)
    return np.ascontiguousarray(words), np.ascontiguousarray(byte.astype(np.uint8).reshape(k // 512, 16, n))


def unpack_weight(words, scales, fmt):
    g, _, n = scales.shape
    words = np.ascontiguousarray(words).reshape(g, 128, n, -1)
    if fmt == "e4m3":
        vals = words.view(ml_dtypes.float8_e4m3fn).astype(np.float64)
    else:
        nib = np.empty((g, 128, n, 4), np.uint8)
        nib[..., 0::2] = words & 0xF
        nib[..., 1::2] = words >> 4
        vals = E2M1[nib]
    vals = vals * np.repeat(np.exp2(scales.astype(np.float64) - 127.0), 8, axis=1)[..., None]
    return vals.transpose(0, 1, 3, 2).reshape(g * 512, n)


def bf(x):
    return np.asarray(x, np.float32).astype(ml_dtypes.bfloat16)


def planes(Y):
    r, m = Y.shape
    b = f64(bf(Y)).reshape(r // 32, 32, m)
    amax = np.abs(b).max(1)
    byte = np.clip(np.where(amax > 0, np.frexp(amax)[1] - 1 + 127 - 7, 1), 1, 254)
    codes = (b * np.exp2(127.0 - byte)[:, None, :]).reshape(r, m).astype(np.float32).astype(ml_dtypes.float8_e4m3fn).view(np.uint8)
    words = codes.reshape(r // 512, 128, 4, m).transpose(0, 1, 3, 2)
    return np.ascontiguousarray(words), np.ascontiguousarray(byte.astype(np.uint8).reshape(r // 512, 16, m))


K, T, J, N = 512, 512, 512, 512


def setup_inputs():
    n = np.random.standard_normal
    idx = np.stack([np.random.randint(0, T, J) for _ in range(8)])
    idx2 = np.stack([np.random.randint(0, T, J) for _ in range(8)])
    fk = mx_kscale(K)
    wap = pack_weight(n((K, N)) * 1 / np.sqrt(K) * fk[:, None], "e2m1")
    wbp = pack_weight(n((K, N)) * 1 / np.sqrt(K) * fk[:, None], "e4m3")
    return {
        "xt": (n((K, T)) / fk[:, None]).astype(np.float32),
        "wa_words": wap[0],
        "wa_scales": wap[1],
        "wb_words": wbp[0],
        "wb_scales": wbp[1],
        "gm": (np.random.uniform(0.5, 2.0, (N, 1))).astype(np.float32),
        "offs": striped8(idx),
        "offs2": striped8(idx2),
    }


def reference(xt, wa_words, wa_scales, wb_words, wb_scales, gm, offs, offs2):
    idx = unstriped8(offs)
    idx2 = unstriped8(offs2)
    wau = unpack_weight(wa_words, wa_scales, "e2m1")
    wbu = unpack_weight(wb_words, wb_scales, "e4m3")
    xtq = mxq(f64(xt), 0, "e4m3")
    z = wau.T @ xtq
    u = wbu.T @ xtq
    y = f64(gm) * pick8(z, idx, 64) / (1.0 + np.maximum(pick8(u, idx2, 64), 0.0))
    words, scales = planes(y)
    return y, words, scales

@@ -1,0 +1,207 @@
+from contextlib import ExitStack
+
+import concourse.mybir as mybir
+
+K, T, J, N = 512, 512, 512, 512
+FLOPS = 2 * 2 * K * N * T
+
+F32 = mybir.dt.float32
+BF16 = mybir.dt.bfloat16
+I32 = mybir.dt.int32
+U32 = mybir.dt.uint32
+U16 = mybir.dt.uint16
+U8 = mybir.dt.uint8
+FP8X4 = mybir.dt.float8_e4m3fn_x4
+FP4X4 = mybir.dt.float4_e2m1fn_x4
+ALU = mybir.AluOpType
+ACT = mybir.ActivationFunctionType
+
+P = 128
+R = 4
+HALF = T // 2
+U_PIECES = ((0, 256), (256, 256))
+Y_PIECES = ((0, 256), (256, 128), (384, 128))
+
+
+def tile_list_head_divided_by_own_list_pl_kernel(
+    tc, xt, wa_words, wa_scales, wb_words, wb_scales, gm, offs, offs2, out_0, out_1, out_2
+):
+    nc = tc.nc
+    with ExitStack() as ctx:
+        sb = ctx.enter_context(tc.tile_pool(name="sb", bufs=1))
+        ps = ctx.enter_context(tc.psum_pool(name="ps", bufs=1))
+
+        z_list = sb.tile([P, J // 16], U16, name="z_list")
+        u_list = sb.tile([P, J // 16], U16, name="u_list")
+
+        def load_scale_rows(queue, plane, scales):
+            for q in range(4):
+                queue.dma_start(
+                    out=plane[32 * q : 32 * q + 4, :].bitcast(I32),
+                    in_=scales[0, 4 * q : 4 * q + 4, :].bitcast(I32),
+                )
+
+        def deal(engine, dst, src, run):
+            engine.tensor_copy(
+                out=dst.rearrange("p (r c i) -> p c r i", r=R, i=run),
+                in_=src.rearrange("p (c i r) -> p c r i", r=R, i=run),
+            )
+
+        def interleave(engine_copy, dst, src):
+            engine_copy(
+                out=dst.rearrange("p (c i) r -> p c r i", i=4),
+                in_=src.rearrange("p r (c i) -> p c r i", i=4),
+            )
+
+        wb_plane_in = sb.tile([P, N], U8, name="wb_plane_in")
+        wa_plane_in = sb.tile([P, N], U8, name="wa_plane_in")
+        nc.vector.memset(wb_plane_in[:].bitcast(I32), 0)
+        nc.gpsimd.memset(wa_plane_in[:].bitcast(I32), 0)
+        warm_in = sb.tile([P, 1], F32, name="warm_in")
+        warm_out = sb.tile([P, 1], F32, name="warm_out")
+        nc.vector.memset(warm_in[:], 1.0)
+
+        x_rows = xt.rearrange("(p r) t -> p r t", r=R)
+        x_in = [sb.tile([P, R, HALF], F32, name=f"x_in{h}") for h in range(2)]
+        wb_in = sb.tile([P, N], I32, name="wb_in")
+        wa_in = sb.tile([P, 2 * N], U8, name="wa_in")
+        gm_sb = sb.tile([P, R], F32, name="gm_sb")
+        nc.sync.dma_start(out=wb_in[:], in_=wb_words[0].rearrange("p n r -> p (n r)").bitcast(I32))
+        nc.sync.dma_start(out=x_in[0][:], in_=x_rows[:, :, :HALF])
+        nc.sync.dma_start(u_list[:], offs2)
+        load_scale_rows(nc.sync, wb_plane_in, wb_scales)
+        nc.scalar.activation(out=warm_out[:], in_=warm_in[:], func=ACT.Abs_reciprocal_sqrt)
+        nc.sync.dma_start(out=x_in[1][:], in_=x_rows[:, :, HALF:])
+        nc.sync.dma_start(out=wa_in[:].bitcast(I32), in_=wa_words[0].bitcast(I32))
+        load_scale_rows(nc.sync, wa_plane_in, wa_scales)
+        nc.sync.dma_start(z_list[:], offs)
+        nc.sync.dma_start(out=gm_sb[:], in_=gm.rearrange("(p r) o -> p (r o)", r=R))
+
+        wb_codes = sb.tile([P, N], I32, name="wb_codes", align_bytes=64)
+        wb_plane = sb.tile([P, N], U8, name="wb_plane", align_bytes=64)
+        deal(nc.vector, wb_codes[:], wb_in[:], 4)
+        deal(nc.vector, wb_plane[:], wb_plane_in[:], 16)
+
+        x_codes = sb.tile([P, T], U32, name="x_codes", align_bytes=64)
+        x_plane = sb.tile([P, T], U8, name="x_plane", align_bytes=64)
+        u_win = [sb.tile([P, T], F32, name=f"u_win{r}") for r in range(R)]
+        z_win = [sb.tile([P, T], F32, name=f"z_win{r}") for r in range(R)]
+        for h in range(2):
+            cols = slice(h * HALF, (h + 1) * HALF)
+            x_bf = sb.tile([P, HALF, R], BF16, name=f"x_bf{h}", align_bytes=64)
+            split = 192 if h == 0 else HALF
+            interleave(nc.vector.tensor_copy, x_bf[:, :split, :], x_in[h][:, :, :split])
+            if split < HALF:
+                interleave(nc.scalar.copy, x_bf[:, split:, :], x_in[h][:, :, split:])
+            nc.vector.quantize_mx(
+                out=x_codes[:, cols].bitcast(FP8X4),
+                scales=x_plane[:, cols],
+                in_=x_bf[:].rearrange("p t r -> p (t r)"),
+            )
+            per_bank = 2 if h == 0 else 1
+            for b in range(R // per_bank):
+                bank = ps.tile([P, 2, HALF], F32, name=f"u_bank{h}{b}", tag=f"bank{2 * h + b}")
+                for s in range(per_bank):
+                    r = per_bank * b + s
+                    nc.tensor.matmul_mx(
+                        out=bank[:, s, :],
+                        lhsT=wb_codes[:, r * P : (r + 1) * P].bitcast(FP8X4),
+                        lhsT_scale=wb_plane[:, r * P : (r + 1) * P],
+                        rhs=x_codes[:, cols].bitcast(FP8X4),
+                        rhs_scale=x_plane[:, cols],
+                        start=True,
+                        stop=True,
+                    )
+                for s in range(per_bank):
+                    nc.scalar.copy(out=u_win[per_bank * b + s][:, cols], in_=bank[:, s, :])
+
+        wa_codes = sb.tile([P, 2 * N], U8, name="wa_codes", align_bytes=64)
+        wa_plane = sb.tile([P, N], U8, name="wa_plane", align_bytes=64)
+        nc.gpsimd.tensor_copy(
+            out=wa_codes[:].rearrange("p (r m b) -> p m r b", r=R, b=2),
+            in_=wa_in[:].rearrange("p (m r b) -> p m r b", r=R, b=2),
+        )
+        deal(nc.gpsimd, wa_plane[:], wa_plane_in[:], 16)
+
+        z_banks = []
+        for r in range(R):
+            bank = ps.tile([P, T], F32, name=f"z_bank{r}", tag=f"bank{(6 + r) % 8}")
+            nc.tensor.matmul_mx(
+                out=bank[:],
+                lhsT=wa_codes[:, 2 * r * P : 2 * (r + 1) * P].bitcast(FP4X4),
+                lhsT_scale=wa_plane[:, r * P : (r + 1) * P],
+                rhs=x_codes[:].bitcast(FP8X4),
+                rhs_scale=x_plane[:],
+                start=True,
+                stop=True,
+            )
+            z_banks.append(bank)
+
+        factor = {}
+        for i, (j0, w) in enumerate(U_PIECES):
+            for pair in range(2):
+                picked = sb.tile([P, 2, w], F32, name=f"picked{i}{pair}")
+                for s in range(2):
+                    nc.vector.tensor_copy(
+                        picked[:, s, :],
+                        u_win[2 * pair + s][:].indirect(u_list[:, j0 // 16 : (j0 + w) // 16]),
+                    )
+                denom = sb.tile([P, 2 * w], F32, name=f"denom{i}{pair}")
+                nc.vector.tensor_scalar(
+                    out=denom[:],
+                    in0=picked[:].rearrange("p s j -> p (s j)"),
+                    scalar1=0.0,
+                    scalar2=1.0,
+                    op0=ALU.max,
+                    op1=ALU.add,
+                )
+                root = sb.tile([P, 2 * w], F32, name=f"root{i}{pair}")
+                nc.scalar.activation(out=root[:], in_=denom[:], func=ACT.Abs_reciprocal_sqrt)
+                recip = sb.tile([P, 2 * w], F32, name=f"recip{i}{pair}")
+                nc.scalar.activation(out=recip[:], in_=root[:], func=ACT.Square)
+                if i == 0:
+                    for s in range(2):
+                        nc.scalar.copy(out=z_win[2 * pair + s][:], in_=z_banks[2 * pair + s][:])
+                for s in range(2):
+                    factor[(i, 2 * pair + s)] = recip[:, s * w : (s + 1) * w]
+
+        y_codes = sb.tile([P, J], U32, name="y_codes", align_bytes=64)
+        y_plane = sb.tile([P, J], U8, name="y_plane", align_bytes=64)
+        y_rows = out_0.rearrange("(p r) j -> p r j", r=R)
+        words_out = out_1[0].rearrange("p j r -> p (j r)").bitcast(I32)
+        scaled = {}
+        for i, (j0, w) in enumerate(Y_PIECES):
+            cols = slice(j0, j0 + w)
+            up = j0 // 256
+            y = sb.tile([P, R, w], F32, name=f"y{i}")
+            for r in range(R):
+                if (up, r) not in scaled:
+                    f = sb.tile([P, 256], F32, name=f"scaled{up}{r}")
+                    nc.vector.tensor_scalar(
+                        out=f[:], in0=factor[(up, r)], scalar1=gm_sb[:, r : r + 1], scalar2=None, op0=ALU.mult
+                    )
+                    scaled[(up, r)] = f
+            for r in range(R):
+                a = j0 - up * 256
+                nc.vector.tensor_tensor(
+                    y[:, r, :],
+                    z_win[r][:].indirect(z_list[:, j0 // 16 : (j0 + w) // 16]),
+                    scaled[(up, r)][:, a : a + w],
+                    ALU.mult,
+                )
+            nc.sync.dma_start(out=y_rows[:, :, cols], in_=y[:])
+            y_bf = sb.tile([P, w, R], BF16, name=f"y_bf{i}", align_bytes=64)
+            last = i == len(Y_PIECES) - 1
+            interleave(nc.vector.tensor_copy if last else nc.scalar.copy, y_bf[:], y[:])
+            nc.vector.quantize_mx(
+                out=y_codes[:, cols].bitcast(FP8X4),
+                scales=y_plane[:, cols],
+                in_=y_bf[:].rearrange("p j r -> p (j r)"),
+            )
+            nc.sync.dma_start(out=words_out[:, cols], in_=y_codes[:, cols].bitcast(I32))
+        for q in range(4):
+            queue = nc.scalar if q % 2 else nc.sync
+            queue.dma_start(
+                out=out_2[0, 4 * q : 4 * q + 4, :].bitcast(I32),
+                in_=y_plane[32 * q : 32 * q + 4, :].bitcast(I32),
+            )

@@ -49,14 +49,16 @@ def tile_list_head_divided_by_own_list_pl_kernel(
 
         def interleave(engine_copy, dst, src):
             engine_copy(
-                out=dst.rearrange("p (c i) r -> p c r i", i=4),
-                in_=src.rearrange("p r (c i) -> p c r i", i=4),
+                out=dst,
+                in_=src.rearrange("p r c -> p c r"),
             )
 
         wb_plane_in = sb.tile([P, N], U8, name="wb_plane_in")
-        wa_plane_in = sb.tile([P, N], U8, name="wa_plane_in")
+        wa_stage = sb.tile([P, 3 * N], U8, name="wa_stage", tag="wa_stage")
+        wa_in = wa_stage[:, : 2 * N]
+        wa_plane_in = wa_stage[:, 2 * N :]
         nc.vector.memset(wb_plane_in[:].bitcast(I32), 0)
-        nc.gpsimd.memset(wa_plane_in[:].bitcast(I32), 0)
+        nc.gpsimd.memset(wa_plane_in.bitcast(I32), 0)
         warm_in = sb.tile([P, 1], F32, name="warm_in")
         warm_out = sb.tile([P, 1], F32, name="warm_out")
         nc.vector.memset(warm_in[:], 1.0)
@@ -64,17 +66,16 @@ def tile_list_head_divided_by_own_list_pl_kernel(
         x_rows = xt.rearrange("(p r) t -> p r t", r=R)
         x_in = [sb.tile([P, R, HALF], F32, name=f"x_in{h}") for h in range(2)]
         wb_in = sb.tile([P, N], I32, name="wb_in")
-        wa_in = sb.tile([P, 2 * N], U8, name="wa_in")
         gm_sb = sb.tile([P, R], F32, name="gm_sb")
-        nc.sync.dma_start(out=wb_in[:], in_=wb_words[0].rearrange("p n r -> p (n r)").bitcast(I32))
-        nc.sync.dma_start(out=x_in[0][:], in_=x_rows[:, :, :HALF])
         nc.sync.dma_start(u_list[:], offs2)
+        nc.sync.dma_start(out=wb_in[:], in_=wb_words[0].rearrange("p n r -> p (n r)").bitcast(I32))
+        nc.sync.dma_start(z_list[:], offs)
         load_scale_rows(nc.sync, wb_plane_in, wb_scales)
         nc.scalar.activation(out=warm_out[:], in_=warm_in[:], func=ACT.Abs_reciprocal_sqrt)
+        nc.sync.dma_start(out=x_in[0][:], in_=x_rows[:, :, :HALF])
         nc.sync.dma_start(out=x_in[1][:], in_=x_rows[:, :, HALF:])
-        nc.sync.dma_start(out=wa_in[:].bitcast(I32), in_=wa_words[0].bitcast(I32))
+        nc.sync.dma_start(out=wa_in.bitcast(I32), in_=wa_words[0].bitcast(I32))
         load_scale_rows(nc.sync, wa_plane_in, wa_scales)
-        nc.sync.dma_start(z_list[:], offs)
         nc.sync.dma_start(out=gm_sb[:], in_=gm.rearrange("(p r) o -> p (r o)", r=R))
 
         wb_codes = sb.tile([P, N], I32, name="wb_codes", align_bytes=64)
@@ -117,11 +118,8 @@ def tile_list_head_divided_by_own_list_pl_kernel(
 
         wa_codes = sb.tile([P, 2 * N], U8, name="wa_codes", align_bytes=64)
         wa_plane = sb.tile([P, N], U8, name="wa_plane", align_bytes=64)
-        nc.gpsimd.tensor_copy(
-            out=wa_codes[:].rearrange("p (r m b) -> p m r b", r=R, b=2),
-            in_=wa_in[:].rearrange("p (m r b) -> p m r b", r=R, b=2),
-        )
-        deal(nc.gpsimd, wa_plane[:], wa_plane_in[:], 16)
+        deal(nc.vector, wa_codes[:].bitcast(U16), wa_in.bitcast(U16), 8)
+        deal(nc.vector, wa_plane[:], wa_plane_in, 16)
 
         z_banks = []
         for r in range(R):
@@ -138,25 +136,23 @@ def tile_list_head_divided_by_own_list_pl_kernel(
             z_banks.append(bank)
 
         factor = {}
+        picked = sb.tile([P, R * J], F32, name="picked", tag="wa_stage")
         for i, (j0, w) in enumerate(U_PIECES):
             for pair in range(2):
-                picked = sb.tile([P, 2, w], F32, name=f"picked{i}{pair}")
+                g0 = (2 * i + pair) * 2 * w
                 for s in range(2):
                     nc.vector.tensor_copy(
-                        picked[:, s, :],
+                        picked[:, g0 + s * w : g0 + (s + 1) * w],
                         u_win[2 * pair + s][:].indirect(u_list[:, j0 // 16 : (j0 + w) // 16]),
                     )
                 denom = sb.tile([P, 2 * w], F32, name=f"denom{i}{pair}")
-                nc.vector.tensor_scalar(
-                    out=denom[:],
-                    in0=picked[:].rearrange("p s j -> p (s j)"),
-                    scalar1=0.0,
-                    scalar2=1.0,
-                    op0=ALU.max,
-                    op1=ALU.add,
-                )
+                flat = picked[:, g0 : g0 + 2 * w]
+                if i == 0:
+                    nc.vector.tensor_scalar(out=denom[:], in0=flat, scalar1=0.0, scalar2=None, op0=ALU.max)
+                else:
+                    nc.scalar.activation(out=denom[:], in_=flat, func=ACT.Relu)
                 root = sb.tile([P, 2 * w], F32, name=f"root{i}{pair}")
-                nc.scalar.activation(out=root[:], in_=denom[:], func=ACT.Abs_reciprocal_sqrt)
+                nc.scalar.activation(out=root[:], in_=denom[:], func=ACT.Abs_reciprocal_sqrt, bias=1.0)
                 recip = sb.tile([P, 2 * w], F32, name=f"recip{i}{pair}")
                 nc.scalar.activation(out=recip[:], in_=root[:], func=ACT.Square)
                 if i == 0:

@@ -16,6 +16,7 @@ FP4X4 = mybir.dt.float4_e2m1fn_x4
 ALU = mybir.AluOpType
 ACT = mybir.ActivationFunctionType
 
+F32_MAX = 3.4028234663852886e38
 P = 128
 R = 4
 HALF = T // 2
@@ -29,6 +30,7 @@ def tile_list_head_divided_by_own_list_pl_kernel(
     nc = tc.nc
     with ExitStack() as ctx:
         sb = ctx.enter_context(tc.tile_pool(name="sb", bufs=1))
+        shared = ctx.enter_context(tc.tile_pool(name="shared", bufs=1))
         ps = ctx.enter_context(tc.psum_pool(name="ps", bufs=1))
 
         z_list = sb.tile([P, J // 16], U16, name="z_list")
@@ -64,7 +66,10 @@ def tile_list_head_divided_by_own_list_pl_kernel(
         nc.vector.memset(warm_in[:], 1.0)
 
         x_rows = xt.rearrange("(p r) t -> p r t", r=R)
-        x_in = [sb.tile([P, R, HALF], F32, name=f"x_in{h}") for h in range(2)]
+        x_in = [
+            sb.tile([P, R, HALF], F32, name="x_in0"),
+            shared.tile([P, R, HALF], F32, name="x_in1", offset=1024),
+        ]
         wb_in = sb.tile([P, N], I32, name="wb_in")
         gm_sb = sb.tile([P, R], F32, name="gm_sb")
         nc.sync.dma_start(u_list[:], offs2)
@@ -85,36 +90,35 @@ def tile_list_head_divided_by_own_list_pl_kernel(
 
         x_codes = sb.tile([P, T], U32, name="x_codes", align_bytes=64)
         x_plane = sb.tile([P, T], U8, name="x_plane", align_bytes=64)
-        u_win = [sb.tile([P, T], F32, name=f"u_win{r}") for r in range(R)]
+        u_win = [shared.tile([P, T], F32, name=f"u_win{r}", offset=4 * T * r) for r in range(R)]
         z_win = [sb.tile([P, T], F32, name=f"z_win{r}") for r in range(R)]
         for h in range(2):
             cols = slice(h * HALF, (h + 1) * HALF)
             x_bf = sb.tile([P, HALF, R], BF16, name=f"x_bf{h}", align_bytes=64)
-            split = 192 if h == 0 else HALF
+            split = 176
             interleave(nc.vector.tensor_copy, x_bf[:, :split, :], x_in[h][:, :, :split])
-            if split < HALF:
-                interleave(nc.scalar.copy, x_bf[:, split:, :], x_in[h][:, :, split:])
+            interleave(nc.scalar.copy, x_bf[:, split:, :], x_in[h][:, :, split:])
             nc.vector.quantize_mx(
                 out=x_codes[:, cols].bitcast(FP8X4),
                 scales=x_plane[:, cols],
                 in_=x_bf[:].rearrange("p t r -> p (t r)"),
             )
-            per_bank = 2 if h == 0 else 1
-            for b in range(R // per_bank):
-                bank = ps.tile([P, 2, HALF], F32, name=f"u_bank{h}{b}", tag=f"bank{2 * h + b}")
-                for s in range(per_bank):
-                    r = per_bank * b + s
-                    nc.tensor.matmul_mx(
-                        out=bank[:, s, :],
-                        lhsT=wb_codes[:, r * P : (r + 1) * P].bitcast(FP8X4),
-                        lhsT_scale=wb_plane[:, r * P : (r + 1) * P],
-                        rhs=x_codes[:, cols].bitcast(FP8X4),
-                        rhs_scale=x_plane[:, cols],
-                        start=True,
-                        stop=True,
-                    )
-                for s in range(per_bank):
-                    nc.scalar.copy(out=u_win[per_bank * b + s][:, cols], in_=bank[:, s, :])
+        def u_product(bank, r, cols):
+            nc.tensor.matmul_mx(
+                out=bank,
+                lhsT=wb_codes[:, r * P : (r + 1) * P].bitcast(FP8X4),
+                lhsT_scale=wb_plane[:, r * P : (r + 1) * P],
+                rhs=x_codes[:, cols].bitcast(FP8X4),
+                rhs_scale=x_plane[:, cols],
+                start=True,
+                stop=True,
+            )
+
+        parts = [(r, 0, HALF) for r in range(R - 1)] + [(r, HALF, T) for r in range(R - 1)] + [(R - 1, 0, T)]
+        for b, (r, t0, t1) in enumerate(parts):
+            bank = ps.tile([P, T], F32, name=f"u_bank{b}", tag=f"bank{b}")
+            u_product(bank[:, : t1 - t0], r, slice(t0, t1))
+            nc.scalar.copy(out=u_win[r][:, t0:t1], in_=bank[:, : t1 - t0])
 
         wa_codes = sb.tile([P, 2 * N], U8, name="wa_codes", align_bytes=64)
         wa_plane = sb.tile([P, N], U8, name="wa_plane", align_bytes=64)
@@ -123,7 +127,7 @@ def tile_list_head_divided_by_own_list_pl_kernel(
 
         z_banks = []
         for r in range(R):
-            bank = ps.tile([P, T], F32, name=f"z_bank{r}", tag=f"bank{(6 + r) % 8}")
+            bank = ps.tile([P, T], F32, name=f"z_bank{r}", tag=f"bank{(7 + r) % 8}")
             nc.tensor.matmul_mx(
                 out=bank[:],
                 lhsT=wa_codes[:, 2 * r * P : 2 * (r + 1) * P].bitcast(FP4X4),
@@ -147,8 +151,10 @@ def tile_list_head_divided_by_own_list_pl_kernel(
                     )
                 denom = sb.tile([P, 2 * w], F32, name=f"denom{i}{pair}")
                 flat = picked[:, g0 : g0 + 2 * w]
-                if i == 0:
-                    nc.vector.tensor_scalar(out=denom[:], in0=flat, scalar1=0.0, scalar2=None, op0=ALU.max)
+                if (i, pair) != (1, 1):
+                    nc.gpsimd.tensor_scalar(
+                        out=denom[:], in0=flat, scalar1=F32_MAX, scalar2=0.0, op0=ALU.min, op1=ALU.max
+                    )
                 else:
                     nc.scalar.activation(out=denom[:], in_=flat, func=ACT.Relu)
                 root = sb.tile([P, 2 * w], F32, name=f"root{i}{pair}")
@@ -186,7 +192,7 @@ def tile_list_head_divided_by_own_list_pl_kernel(
                     ALU.mult,
                 )
             nc.sync.dma_start(out=y_rows[:, :, cols], in_=y[:])
-            y_bf = sb.tile([P, w, R], BF16, name=f"y_bf{i}", align_bytes=64)
+            y_bf = sb.tile([P, w, R], BF16, name=f"y_bf{i}", tag=f"y_bf{i % 2}", align_bytes=64)
             last = i == len(Y_PIECES) - 1
             interleave(nc.vector.tensor_copy if last else nc.scalar.copy, y_bf[:], y[:])
             nc.vector.quantize_mx(
@@ -194,9 +200,11 @@ def tile_list_head_divided_by_own_list_pl_kernel(
                 scales=y_plane[:, cols],
                 in_=y_bf[:].rearrange("p j r -> p (j r)"),
             )
-            nc.sync.dma_start(out=words_out[:, cols], in_=y_codes[:, cols].bitcast(I32))
+            if i == 0:
+                nc.sync.dma_start(out=words_out[:, cols], in_=y_codes[:, cols].bitcast(I32))
+        nc.sync.dma_start(out=words_out[:, 256:], in_=y_codes[:, 256:].bitcast(I32))
         for q in range(4):
-            queue = nc.scalar if q % 2 else nc.sync
+            queue = nc.sync if q == 3 else nc.scalar
             queue.dma_start(
                 out=out_2[0, 4 * q : 4 * q + 4, :].bitcast(I32),
                 in_=y_plane[32 * q : 32 * q + 4, :].bitcast(I32),

@@ -20,6 +20,8 @@ F32_MAX = 3.4028234663852886e38
 P = 128
 R = 4
 HALF = T // 2
+QUARTER = T // 4
+X_PIECES = ((0, HALF, 176), (HALF, QUARTER, 0), (HALF + QUARTER, QUARTER, QUARTER))
 U_PIECES = ((0, 256), (256, 256))
 Y_PIECES = ((0, 256), (256, 128), (384, 128))
 
@@ -51,8 +53,8 @@ def tile_list_head_divided_by_own_list_pl_kernel(
 
         def interleave(engine_copy, dst, src):
             engine_copy(
-                out=dst,
-                in_=src.rearrange("p r c -> p c r"),
+                out=dst.rearrange("p (c i) r -> p c r i", i=4),
+                in_=src.rearrange("p r (c i) -> p c r i", i=4),
             )
 
         wb_plane_in = sb.tile([P, N], U8, name="wb_plane_in")
@@ -68,7 +70,8 @@ def tile_list_head_divided_by_own_list_pl_kernel(
         x_rows = xt.rearrange("(p r) t -> p r t", r=R)
         x_in = [
             sb.tile([P, R, HALF], F32, name="x_in0"),
-            shared.tile([P, R, HALF], F32, name="x_in1", offset=1024),
+            shared.tile([P, R, QUARTER], F32, name="x_in1", offset=1024),
+            sb.tile([P, R, QUARTER], F32, name="x_in2"),
         ]
         wb_in = sb.tile([P, N], I32, name="wb_in")
         gm_sb = sb.tile([P, R], F32, name="gm_sb")
@@ -77,8 +80,8 @@ def tile_list_head_divided_by_own_list_pl_kernel(
         nc.sync.dma_start(z_list[:], offs)
         load_scale_rows(nc.sync, wb_plane_in, wb_scales)
         nc.scalar.activation(out=warm_out[:], in_=warm_in[:], func=ACT.Abs_reciprocal_sqrt)
-        nc.sync.dma_start(out=x_in[0][:], in_=x_rows[:, :, :HALF])
-        nc.sync.dma_start(out=x_in[1][:], in_=x_rows[:, :, HALF:])
+        for x_piece, (t0, w, split) in zip(x_in, X_PIECES):
+            nc.sync.dma_start(out=x_piece[:], in_=x_rows[:, :, t0 : t0 + w])
         nc.sync.dma_start(out=wa_in.bitcast(I32), in_=wa_words[0].bitcast(I32))
         load_scale_rows(nc.sync, wa_plane_in, wa_scales)
         nc.sync.dma_start(out=gm_sb[:], in_=gm.rearrange("(p r) o -> p (r o)", r=R))
@@ -92,12 +95,13 @@ def tile_list_head_divided_by_own_list_pl_kernel(
         x_plane = sb.tile([P, T], U8, name="x_plane", align_bytes=64)
         u_win = [shared.tile([P, T], F32, name=f"u_win{r}", offset=4 * T * r) for r in range(R)]
         z_win = [sb.tile([P, T], F32, name=f"z_win{r}") for r in range(R)]
-        for h in range(2):
-            cols = slice(h * HALF, (h + 1) * HALF)
-            x_bf = sb.tile([P, HALF, R], BF16, name=f"x_bf{h}", align_bytes=64)
-            split = 176
-            interleave(nc.vector.tensor_copy, x_bf[:, :split, :], x_in[h][:, :, :split])
-            interleave(nc.scalar.copy, x_bf[:, split:, :], x_in[h][:, :, split:])
+        for h, (t0, w, split) in enumerate(X_PIECES):
+            cols = slice(t0, t0 + w)
+            x_bf = sb.tile([P, w, R], BF16, name=f"x_bf{h}", tag=f"x_bf{h}", align_bytes=64)
+            if split > 0:
+                interleave(nc.vector.tensor_copy, x_bf[:, :split, :], x_in[h][:, :, :split])
+            if split < w:
+                interleave(nc.scalar.copy, x_bf[:, split:, :], x_in[h][:, :, split:])
             nc.vector.quantize_mx(
                 out=x_codes[:, cols].bitcast(FP8X4),
                 scales=x_plane[:, cols],
@@ -114,10 +118,13 @@ def tile_list_head_divided_by_own_list_pl_kernel(
                 stop=True,
             )
 
-        parts = [(r, 0, HALF) for r in range(R - 1)] + [(r, HALF, T) for r in range(R - 1)] + [(R - 1, 0, T)]
-        for b, (r, t0, t1) in enumerate(parts):
+        three = HALF + QUARTER
+        parts = [(0, (0, HALF)), (1, (0, HALF)), (0, (HALF, three, T)), (1, (HALF, T)), (2, (0, T)), (3, (0, T))]
+        for b, (r, edges) in enumerate(parts):
             bank = ps.tile([P, T], F32, name=f"u_bank{b}", tag=f"bank{b}")
-            u_product(bank[:, : t1 - t0], r, slice(t0, t1))
+            t0, t1 = edges[0], edges[-1]
+            for a, e in zip(edges[:-1], edges[1:]):
+                u_product(bank[:, a - t0 : e - t0], r, slice(a, e))
             nc.scalar.copy(out=u_win[r][:, t0:t1], in_=bank[:, : t1 - t0])
 
         wa_codes = sb.tile([P, 2 * N], U8, name="wa_codes", align_bytes=64)
@@ -127,7 +134,7 @@ def tile_list_head_divided_by_own_list_pl_kernel(
 
         z_banks = []
         for r in range(R):
-            bank = ps.tile([P, T], F32, name=f"z_bank{r}", tag=f"bank{(7 + r) % 8}")
+            bank = ps.tile([P, T], F32, name=f"z_bank{r}", tag=f"bank{(6 + r) % 8}")
             nc.tensor.matmul_mx(
                 out=bank[:],
                 lhsT=wa_codes[:, 2 * r * P : 2 * (r + 1) * P].bitcast(FP4X4),
@@ -149,16 +156,17 @@ def tile_list_head_divided_by_own_list_pl_kernel(
                         picked[:, g0 + s * w : g0 + (s + 1) * w],
                         u_win[2 * pair + s][:].indirect(u_list[:, j0 // 16 : (j0 + w) // 16]),
                     )
-                denom = sb.tile([P, 2 * w], F32, name=f"denom{i}{pair}")
+                denom_tile = sb.tile([P, 2 * w], F32, name=f"denom{i}{pair}")
+                denom = denom_tile[:]
                 flat = picked[:, g0 : g0 + 2 * w]
                 if (i, pair) != (1, 1):
                     nc.gpsimd.tensor_scalar(
-                        out=denom[:], in0=flat, scalar1=F32_MAX, scalar2=0.0, op0=ALU.min, op1=ALU.max
+                        out=denom, in0=flat, scalar1=F32_MAX, scalar2=0.0, op0=ALU.min, op1=ALU.max
                     )
                 else:
-                    nc.scalar.activation(out=denom[:], in_=flat, func=ACT.Relu)
+                    nc.scalar.activation(out=denom, in_=flat, func=ACT.Relu)
                 root = sb.tile([P, 2 * w], F32, name=f"root{i}{pair}")
-                nc.scalar.activation(out=root[:], in_=denom[:], func=ACT.Abs_reciprocal_sqrt, bias=1.0)
+                nc.scalar.activation(out=root[:], in_=denom, func=ACT.Abs_reciprocal_sqrt, bias=1.0)
                 recip = sb.tile([P, 2 * w], F32, name=f"recip{i}{pair}")
                 nc.scalar.activation(out=recip[:], in_=root[:], func=ACT.Square)
                 if i == 0:

from contextlib import ExitStack

import concourse.mybir as mybir

K, T, J, N = 512, 512, 512, 512
FLOPS = 2 * 2 * K * N * T

F32 = mybir.dt.float32
BF16 = mybir.dt.bfloat16
I32 = mybir.dt.int32
U32 = mybir.dt.uint32
U16 = mybir.dt.uint16
U8 = mybir.dt.uint8
FP8X4 = mybir.dt.float8_e4m3fn_x4
FP4X4 = mybir.dt.float4_e2m1fn_x4
ALU = mybir.AluOpType
ACT = mybir.ActivationFunctionType

F32_MAX = 3.4028234663852886e38
P = 128
R = 4
HALF = T // 2
QUARTER = T // 4
X_PIECES = ((0, HALF, 176), (HALF, QUARTER, 0), (HALF + QUARTER, QUARTER, QUARTER))
U_PIECES = ((0, 256), (256, 256))
Y_PIECES = ((0, 256), (256, 128), (384, 128))


def tile_list_head_divided_by_own_list_pl_kernel(
    tc, xt, wa_words, wa_scales, wb_words, wb_scales, gm, offs, offs2, out_0, out_1, out_2
):
    nc = tc.nc
    with ExitStack() as ctx:
        sb = ctx.enter_context(tc.tile_pool(name="sb", bufs=1))
        shared = ctx.enter_context(tc.tile_pool(name="shared", bufs=1))
        ps = ctx.enter_context(tc.psum_pool(name="ps", bufs=1))

        z_list = sb.tile([P, J // 16], U16, name="z_list")
        u_list = sb.tile([P, J // 16], U16, name="u_list")

        def load_scale_rows(queue, plane, scales):
            for q in range(4):
                queue.dma_start(
                    out=plane[32 * q : 32 * q + 4, :].bitcast(I32),
                    in_=scales[0, 4 * q : 4 * q + 4, :].bitcast(I32),
                )

        def deal(engine, dst, src, run):
            engine.tensor_copy(
                out=dst.rearrange("p (r c i) -> p c r i", r=R, i=run),
                in_=src.rearrange("p (c i r) -> p c r i", r=R, i=run),
            )

        def interleave(engine_copy, dst, src):
            engine_copy(
                out=dst.rearrange("p (c i) r -> p c r i", i=4),
                in_=src.rearrange("p r (c i) -> p c r i", i=4),
            )

        wb_plane_in = sb.tile([P, N], U8, name="wb_plane_in")
        wa_stage = sb.tile([P, 3 * N], U8, name="wa_stage", tag="wa_stage")
        wa_in = wa_stage[:, : 2 * N]
        wa_plane_in = wa_stage[:, 2 * N :]
        nc.vector.memset(wb_plane_in[:].bitcast(I32), 0)
        nc.gpsimd.memset(wa_plane_in.bitcast(I32), 0)
        warm_in = sb.tile([P, 1], F32, name="warm_in")
        warm_out = sb.tile([P, 1], F32, name="warm_out")
        nc.vector.memset(warm_in[:], 1.0)

        x_rows = xt.rearrange("(p r) t -> p r t", r=R)
        x_in = [
            sb.tile([P, R, HALF], F32, name="x_in0"),
            shared.tile([P, R, QUARTER], F32, name="x_in1", offset=1024),
            sb.tile([P, R, QUARTER], F32, name="x_in2"),
        ]
        wb_in = sb.tile([P, N], I32, name="wb_in")
        gm_sb = sb.tile([P, R], F32, name="gm_sb")
        nc.sync.dma_start(u_list[:], offs2)
        nc.sync.dma_start(out=wb_in[:], in_=wb_words[0].rearrange("p n r -> p (n r)").bitcast(I32))
        nc.sync.dma_start(z_list[:], offs)
        load_scale_rows(nc.sync, wb_plane_in, wb_scales)
        nc.scalar.activation(out=warm_out[:], in_=warm_in[:], func=ACT.Abs_reciprocal_sqrt)
        for x_piece, (t0, w, split) in zip(x_in, X_PIECES):
            nc.sync.dma_start(out=x_piece[:], in_=x_rows[:, :, t0 : t0 + w])
        nc.sync.dma_start(out=wa_in.bitcast(I32), in_=wa_words[0].bitcast(I32))
        load_scale_rows(nc.sync, wa_plane_in, wa_scales)
        nc.sync.dma_start(out=gm_sb[:], in_=gm.rearrange("(p r) o -> p (r o)", r=R))

        wb_codes = sb.tile([P, N], I32, name="wb_codes", align_bytes=64)
        wb_plane = sb.tile([P, N], U8, name="wb_plane", align_bytes=64)
        deal(nc.vector, wb_codes[:], wb_in[:], 4)
        deal(nc.vector, wb_plane[:], wb_plane_in[:], 16)

        x_codes = sb.tile([P, T], U32, name="x_codes", align_bytes=64)
        x_plane = sb.tile([P, T], U8, name="x_plane", align_bytes=64)
        u_win = [shared.tile([P, T], F32, name=f"u_win{r}", offset=4 * T * r) for r in range(R)]
        z_win = [sb.tile([P, T], F32, name=f"z_win{r}") for r in range(R)]
        for h, (t0, w, split) in enumerate(X_PIECES):
            cols = slice(t0, t0 + w)
            x_bf = sb.tile([P, w, R], BF16, name=f"x_bf{h}", tag=f"x_bf{h}", align_bytes=64)
            if split > 0:
                interleave(nc.vector.tensor_copy, x_bf[:, :split, :], x_in[h][:, :, :split])
            if split < w:
                interleave(nc.scalar.copy, x_bf[:, split:, :], x_in[h][:, :, split:])
            nc.vector.quantize_mx(
                out=x_codes[:, cols].bitcast(FP8X4),
                scales=x_plane[:, cols],
                in_=x_bf[:].rearrange("p t r -> p (t r)"),
            )
        def u_product(bank, r, cols):
            nc.tensor.matmul_mx(
                out=bank,
                lhsT=wb_codes[:, r * P : (r + 1) * P].bitcast(FP8X4),
                lhsT_scale=wb_plane[:, r * P : (r + 1) * P],
                rhs=x_codes[:, cols].bitcast(FP8X4),
                rhs_scale=x_plane[:, cols],
                start=True,
                stop=True,
            )

        three = HALF + QUARTER
        parts = [(0, (0, HALF)), (1, (0, HALF)), (0, (HALF, three, T)), (1, (HALF, T)), (2, (0, T)), (3, (0, T))]
        for b, (r, edges) in enumerate(parts):
            bank = ps.tile([P, T], F32, name=f"u_bank{b}", tag=f"bank{b}")
            t0, t1 = edges[0], edges[-1]
            for a, e in zip(edges[:-1], edges[1:]):
                u_product(bank[:, a - t0 : e - t0], r, slice(a, e))
            nc.scalar.copy(out=u_win[r][:, t0:t1], in_=bank[:, : t1 - t0])

        wa_codes = sb.tile([P, 2 * N], U8, name="wa_codes", align_bytes=64)
        wa_plane = sb.tile([P, N], U8, name="wa_plane", align_bytes=64)
        deal(nc.vector, wa_codes[:].bitcast(U16), wa_in.bitcast(U16), 8)
        deal(nc.vector, wa_plane[:], wa_plane_in, 16)

        z_banks = []
        for r in range(R):
            bank = ps.tile([P, T], F32, name=f"z_bank{r}", tag=f"bank{(6 + r) % 8}")
            nc.tensor.matmul_mx(
                out=bank[:],
                lhsT=wa_codes[:, 2 * r * P : 2 * (r + 1) * P].bitcast(FP4X4),
                lhsT_scale=wa_plane[:, r * P : (r + 1) * P],
                rhs=x_codes[:].bitcast(FP8X4),
                rhs_scale=x_plane[:],
                start=True,
                stop=True,
            )
            z_banks.append(bank)

        factor = {}
        picked = sb.tile([P, R * J], F32, name="picked", tag="wa_stage")
        for i, (j0, w) in enumerate(U_PIECES):
            for pair in range(2):
                g0 = (2 * i + pair) * 2 * w
                for s in range(2):
                    nc.vector.tensor_copy(
                        picked[:, g0 + s * w : g0 + (s + 1) * w],
                        u_win[2 * pair + s][:].indirect(u_list[:, j0 // 16 : (j0 + w) // 16]),
                    )
                denom_tile = sb.tile([P, 2 * w], F32, name=f"denom{i}{pair}")
                denom = denom_tile[:]
                flat = picked[:, g0 : g0 + 2 * w]
                if (i, pair) != (1, 1):
                    nc.gpsimd.tensor_scalar(
                        out=denom, in0=flat, scalar1=F32_MAX, scalar2=0.0, op0=ALU.min, op1=ALU.max
                    )
                else:
                    nc.scalar.activation(out=denom, in_=flat, func=ACT.Relu)
                root = sb.tile([P, 2 * w], F32, name=f"root{i}{pair}")
                nc.scalar.activation(out=root[:], in_=denom, func=ACT.Abs_reciprocal_sqrt, bias=1.0)
                recip = sb.tile([P, 2 * w], F32, name=f"recip{i}{pair}")
                nc.scalar.activation(out=recip[:], in_=root[:], func=ACT.Square)
                if i == 0:
                    for s in range(2):
                        nc.scalar.copy(out=z_win[2 * pair + s][:], in_=z_banks[2 * pair + s][:])
                for s in range(2):
                    factor[(i, 2 * pair + s)] = recip[:, s * w : (s + 1) * w]

        y_codes = sb.tile([P, J], U32, name="y_codes", align_bytes=64)
        y_plane = sb.tile([P, J], U8, name="y_plane", align_bytes=64)
        y_rows = out_0.rearrange("(p r) j -> p r j", r=R)
        words_out = out_1[0].rearrange("p j r -> p (j r)").bitcast(I32)
        scaled = {}
        for i, (j0, w) in enumerate(Y_PIECES):
            cols = slice(j0, j0 + w)
            up = j0 // 256
            y = sb.tile([P, R, w], F32, name=f"y{i}")
            for r in range(R):
                if (up, r) not in scaled:
                    f = sb.tile([P, 256], F32, name=f"scaled{up}{r}")
                    nc.vector.tensor_scalar(
                        out=f[:], in0=factor[(up, r)], scalar1=gm_sb[:, r : r + 1], scalar2=None, op0=ALU.mult
                    )
                    scaled[(up, r)] = f
            for r in range(R):
                a = j0 - up * 256
                nc.vector.tensor_tensor(
                    y[:, r, :],
                    z_win[r][:].indirect(z_list[:, j0 // 16 : (j0 + w) // 16]),
                    scaled[(up, r)][:, a : a + w],
                    ALU.mult,
                )
            nc.sync.dma_start(out=y_rows[:, :, cols], in_=y[:])
            y_bf = sb.tile([P, w, R], BF16, name=f"y_bf{i}", tag=f"y_bf{i % 2}", align_bytes=64)
            last = i == len(Y_PIECES) - 1
            interleave(nc.vector.tensor_copy if last else nc.scalar.copy, y_bf[:], y[:])
            nc.vector.quantize_mx(
                out=y_codes[:, cols].bitcast(FP8X4),
                scales=y_plane[:, cols],
                in_=y_bf[:].rearrange("p j r -> p (j r)"),
            )
            if i == 0:
                nc.sync.dma_start(out=words_out[:, cols], in_=y_codes[:, cols].bitcast(I32))
        nc.sync.dma_start(out=words_out[:, 256:], in_=y_codes[:, 256:].bitcast(I32))
        for q in range(4):
            queue = nc.sync if q == 3 else nc.scalar
            queue.dma_start(
                out=out_2[0, 4 * q : 4 * q + 4, :].bitcast(I32),
                in_=y_plane[32 * q : 32 * q + 4, :].bitcast(I32),
            )
